import numpy as np
import ml_dtypes


def mxq(x, axis, fmt="e4m3"):
    dtype, down = {"e4m3": (ml_dtypes.float8_e4m3fn, 7), "e5m2": (ml_dtypes.float8_e5m2, 14)}[fmt]
    v = np.moveaxis(np.asarray(x, np.float32).astype(ml_dtypes.bfloat16).astype(np.float64), axis, -1)
    blocks = v.reshape(v.shape[:-1] + (-1, 32))
    amax = np.abs(blocks).max(-1, keepdims=True)
    byte = np.maximum(np.where(amax > 0, np.frexp(amax)[1] - 1 + 127, 0) - down, 1)
    scale = np.exp2(byte - 127.0)
    codes = (blocks / scale).astype(np.float32).astype(dtype).astype(np.float64)
    return np.moveaxis((codes * scale).reshape(v.shape), -1, axis)


WIDE = False


def mx_kscale(k):
    if not WIDE:
        return np.ones(k)
    levels = np.array([30, -30])
    if k % 512:
        return np.exp2(np.random.permutation(np.resize(levels, k // 32))).repeat(32)
    a = np.empty((k // 512, 16))
    for p in range(k // 512):
        a[p, :8] = np.random.permutation(np.resize(levels, 8))
        for g in range(8):
            far = levels[np.abs(levels - a[p, g]) >= 10]
            a[p, g + 8] = far[np.random.randint(len(far))]
    return np.exp2(a.ravel()).repeat(32)


def f64(x):
    return np.asarray(x).astype(np.float64)


def striped(idx):
    return np.tile(idx.reshape(-1, 16).T, (8, 1)).astype(np.uint16)


def unstriped(offs):
    return offs[:16].T.reshape(-1).astype(np.int64)


E2M1 = np.array([0.0, 0.5, 1.0, 1.5, 2.0, 3.0, 4.0, 6.0, -0.0, -0.5, -1.0, -1.5, -2.0, -3.0, -4.0, -6.0])


def pack_weight(w, fmt):
    k, n = w.shape
    w = f64(np.asarray(w, np.float32).astype(ml_dtypes.bfloat16)).reshape(k // 32, 32, n)
    amax = np.abs(w).max(1)
    if fmt == "e4m3":
        byte = np.frexp(amax)[1] - 1 + 127 - 7
    elif fmt == "e5m2":
        byte = np.frexp(amax)[1] - 1 + 127 - 14
    else:
        mant, ex = np.frexp(amax / 6.0)
        byte = np.where(mant > 0.5, ex, ex - 1) + 127
    byte = np.clip(np.where(amax > 0, byte, 1), 1, 254)
    scaled = (w * np.exp2(127.0 - byte)[:, None, :]).reshape(k, n).astype(np.float32)
    by_word = np.ascontiguousarray(scaled.reshape(k // 512, 128, 4, n).transpose(0, 1, 3, 2))
    if fmt == "e4m3":
        words = by_word.astype(ml_dtypes.float8_e4m3fn).view(np.uint8)
    elif fmt == "e5m2":
        words = by_word.astype(ml_dtypes.float8_e5m2).view(np.uint8)
    else:
        c = by_word.astype(ml_dtypes.float4_e2m1fn).view(np.uint8) & 0xF
        words = (c[..., 0::2] | (c[..., 1::2] << 4)).reshape(k // 512, 128, 2 * n)
    return np.ascontiguousarray(words), np.ascontiguousarray(byte.astype(np.uint8).reshape(k // 512, 16, n))


def unpack_weight(words, scales, fmt):
    g, _, n = scales.shape
    words = np.ascontiguousarray(words).reshape(g, 128, n, -1)
    if fmt == "e4m3":
        vals = words.view(ml_dtypes.float8_e4m3fn).astype(np.float64)
    elif fmt == "e5m2":
        vals = words.view(ml_dtypes.float8_e5m2).astype(np.float64)
    else:
        nib = np.empty((g, 128, n, 4), np.uint8)
        nib[..., 0::2] = words & 0xF
        nib[..., 1::2] = words >> 4
        vals = E2M1[nib]
    vals = vals * np.repeat(np.exp2(scales.astype(np.float64) - 127.0), 8, axis=1)[..., None]
    return vals.transpose(0, 1, 3, 2).reshape(g * 512, n)


def d_silu(v):
    s = 1.0 / (1.0 + np.exp(-np.maximum(v, -700.0)))
    return s * (1.0 + v * (1.0 - s))


K, T, E, C, H, N = 256, 1024, 2, 512, 1024, 512


def by_expert(wq, xq):
    return np.concatenate([wq[e].T @ xq[:, e * C:(e + 1) * C] for e in range(E)], axis=1)


def setup_inputs():
    n = np.random.standard_normal
    s = mx_kscale(N)[:, None]
    u = mx_kscale(H)
    dy = pack_weight(n((N, T)) * s, "e5m2")
    return {
        "dy_words": dy[0],
        "dy_scales": dy[1],
        "a": n((H, E * C)).astype(np.float32),
        "w2": (n((E, N, H)) / np.sqrt(N) / s[None] * u[None, None, :]).astype(np.float32),
        "w1": (n((E, H, K)) / np.sqrt(H) / u[None, :, None]).astype(np.float32),
        "gate": np.tile(np.random.uniform(0.2, 1.0, E * C), (H, 1)).astype(np.float32),
        "offs": striped(np.random.permutation(T)[:E * C]),
    }


def reference(dy_words, dy_scales, a, w2, w1, gate, offs):
    idx = unstriped(offs)
    gq = unpack_weight(dy_words, dy_scales, "e5m2")[:, idx]
    dh = f64(gate) * by_expert(mxq(f64(w2), 1, "e4m3"), gq)
    da = dh * d_silu(f64(a))
    dx = by_expert(mxq(f64(w1), 1, "e4m3"), mxq(da, 0, "e5m2"))
    out = np.zeros((K, T))
    out[:, idx] = dx
    return out

@@ -1,0 +1,210 @@
+from contextlib import ExitStack
+
+import concourse.mybir as mybir
+from concourse.masks import make_identity
+
+K, T, E, C, H, N = 256, 1024, 2, 512, 1024, 512
+FLOPS = 2 * E * C * (N * H + H * K)
+
+F32 = mybir.dt.float32
+BF16 = mybir.dt.bfloat16
+I32 = mybir.dt.int32
+U32 = mybir.dt.uint32
+U16 = mybir.dt.uint16
+U8 = mybir.dt.uint8
+E4M3X4 = mybir.dt.float8_e4m3fn_x4
+E5M2X4 = mybir.dt.float8_e5m2_x4
+ACT = mybir.ActivationFunctionType
+ALU = mybir.AluOpType
+
+P = 128
+PACK = 4
+PASS = P * PACK
+HALVES = H // PASS
+BLOCKS = C // P
+K_TILES = K // P
+PAIRS = BLOCKS // 2
+PAIR_SLOTS = 2 * P
+PAIR = PAIR_SLOTS * PACK
+
+
+def interleaved(dst, src):
+    return (
+        dst.rearrange("p (c i j) -> p c j i", i=4, j=PACK),
+        src.rearrange("p j (c i) -> p c j i", i=4),
+    )
+
+
+def tile_moe_bdx_mlp_silu_kernel(
+    tc, dy_words, dy_scales, a, w2, w1, gate, offs, out
+):
+    nc = tc.nc
+    units = [(e, h) for e in range(E) for h in range(HALVES)]
+
+    with ExitStack() as ctx:
+        keep = ctx.enter_context(tc.tile_pool(name="keep", bufs=1))
+        ring = ctx.enter_context(tc.tile_pool(name="ring", bufs=2))
+        psum = ctx.enter_context(tc.psum_pool(name="psum", bufs=2))
+
+        offsets = keep.tile([P, T // 16], U16, name="offsets")
+        nc.sync.dma_start(offsets[:], offs)
+        words = keep.tile([P, T], U32, name="words")
+        nc.sync.dma_start(words[:].bitcast(I32), dy_words[0].rearrange("p t d -> p (t d)").bitcast(I32))
+
+        plane = keep.tile([P, T], U8, name="plane", align_bytes=64)
+        nc.vector.memset(plane[:].bitcast(I32), 0)
+        for r in range(4):
+            nc.sync.dma_start(plane[:].bitcast(I32)[r:P:32, :], dy_scales[0].bitcast(I32)[r:16:4, :])
+
+        gate_rows = keep.tile([P, P], F32, name="gate_rows")
+        nc.vector.memset(gate_rows[:], 0.0)
+        ident = keep.tile([P, P], F32, name="ident")
+        make_identity(nc, ident[:])
+
+        warm = keep.tile([P, 1], F32, name="warm")
+        nc.scalar.activation(warm[:], ident[:, 0:1], ACT.Silu)
+
+        w2_raw, a_raw, w1_raw = {}, {}, {}
+
+        def load_a(e, h, first, count):
+            tile = keep.tile([P, PACK, count * PAIR_SLOTS], F32, name="a_raw%d%d%d" % (e, h, first))
+            lo = e * C + first * PAIR_SLOTS
+            rows = a[h * PASS : (h + 1) * PASS, lo : lo + count * PAIR_SLOTS]
+            nc.sync.dma_start(tile[:], rows.rearrange("(p j) s -> p j s", j=PACK))
+            for pair in range(count):
+                a_raw[e, h, first + pair] = tile[:, :, pair * PAIR_SLOTS : (pair + 1) * PAIR_SLOTS]
+
+        def load_w2(e, h):
+            w2_raw[e, h] = keep.tile([P, PACK, PASS], F32, name="w2_raw%d%d" % (e, h))
+            cols = w2[e, :, h * PASS : (h + 1) * PASS]
+            nc.sync.dma_start(w2_raw[e, h][:], cols.rearrange("(p j) i -> p j i", j=PACK))
+
+        def load_w1(e, h):
+            w1_raw[e, h] = keep.tile([P, PACK, K], F32, name="w1_raw%d%d" % (e, h))
+            rows = w1[e, h * PASS : (h + 1) * PASS, :]
+            nc.sync.dma_start(w1_raw[e, h][:], rows.rearrange("(p j) k -> p j k", j=PACK))
+
+        load_a(*units[0], 0, 1)
+        load_w2(*units[0])
+        nc.sync.dma_start(gate_rows[0 : E * BLOCKS, :], gate[0:1, :].rearrange("o (b c) -> (o b) c", c=P))
+        load_a(*units[0], 1, 1)
+        for u in range(1, len(units)):
+            load_a(*units[u], 0, PAIRS)
+            load_w2(*units[u])
+            load_w1(*units[u - 1])
+        load_w1(*units[-1])
+
+        lists = [offsets[:, e * C // 16 : (e + 1) * C // 16] for e in range(E)]
+        g_words = [keep.tile([P, C], U32, name="g_words%d" % e, align_bytes=64) for e in range(E)]
+        g_scales = [keep.tile([P, C], U8, name="g_scales%d" % e, align_bytes=64) for e in range(E)]
+        for e in range(E):
+            nc.vector.tensor_copy(g_words[e][:], words[:].indirect(lists[e]))
+        for e in range(E):
+            nc.vector.tensor_copy(g_scales[e][:], plane[:].indirect(lists[e]))
+
+        gate_t = psum.tile([P, C], F32, name="gate_t", tag="dx")
+        nc.tensor.transpose(gate_t[:, 0:P], gate_rows[:], ident[:])
+        gate_col = keep.tile([P, E * BLOCKS], F32, name="gate_col")
+        nc.vector.tensor_scalar(gate_col[:], gate_t[:, 0 : E * BLOCKS], -0.5, None, ALU.mult)
+
+        windows = {0: keep.tile([P, T], F32, name="window0")}
+
+        def quantised(raw, width, name, cast):
+            rounded = ring.tile([P, width * PACK], BF16, name=name + "_bf16", align_bytes=64)
+            cast(*interleaved(rounded[:], raw[:]))
+            codes = ring.tile([P, width], U32, name=name + "_codes", align_bytes=64)
+            scales = ring.tile([P, width], U8, name=name + "_scales", align_bytes=64)
+            nc.vector.quantize_mx(out=codes[:].bitcast(E4M3X4), scales=scales[:], in_=rounded[:])
+            return codes, scales
+
+        w2_q = {units[0]: quantised(w2_raw[units[0]], PASS, "w2", nc.vector.tensor_copy)}
+        dx = {}
+        results = {}
+
+        def scatter(e, kt):
+            nc.vector.tensor_copy(windows[kt][:].indirect(lists[e]), results[e, kt][:])
+
+        for u, (e, h) in enumerate(units):
+            w2_codes, w2_scales = w2_q[e, h]
+            da_codes = ring.tile([P, C], U32, name="da_codes", align_bytes=64)
+            da_scales = ring.tile([P, C], U8, name="da_scales", align_bytes=64)
+            for pair in range(BLOCKS // 2):
+                slots = slice(pair * 2 * P, (pair + 1) * 2 * P)
+                tanh_half = ring.tile([P, PAIR], F32, name="tanh_half", bufs=4)
+                dst, src = interleaved(tanh_half[:], a_raw[e, h, pair])
+                nc.scalar.activation(dst, src, ACT.Tanh, scale=0.5)
+                silu_neg = ring.tile([P, PAIR], F32, name="silu_neg", bufs=4)
+                dst, src = interleaved(silu_neg[:], a_raw[e, h, pair])
+                nc.scalar.activation(dst, src, ACT.Silu, scale=-1.0)
+                last = u + 1 == len(units) and pair + 1 == PAIRS
+                if last:
+                    partial = ring.tile([P, PAIR], F32, name="partial_last", tag="partial", bufs=1)
+                else:
+                    partial = ring.tile([P, PAIR], F32, name="partial_ring")
+                for half_pair in range(2):
+                    b = 2 * pair + half_pair
+                    cols = slice(b * P, (b + 1) * P)
+                    dh_t = psum.tile([P, PASS], F32, name="dh_t", bufs=3)
+                    nc.tensor.matmul_mx(
+                        out=dh_t[:],
+                        lhsT=g_words[e][:, cols].bitcast(E5M2X4),
+                        lhsT_scale=g_scales[e][:, cols],
+                        rhs=w2_codes[:].bitcast(E4M3X4),
+                        rhs_scale=w2_scales[:],
+                        start=True,
+                        stop=True,
+                    )
+                    gated = ring.tile([P, PACK, P], F32, name="gated", bufs=3)
+                    col = e * BLOCKS + b
+                    nc.scalar.activation(
+                        gated[:],
+                        dh_t[:].rearrange("s (p j) -> s j p", j=PACK),
+                        ACT.Copy,
+                        scale=gate_col[:, col : col + 1],
+                    )
+                    dh = psum.tile([P, PACK, P], F32, name="dh", bufs=3)
+                    for j in range(PACK):
+                        nc.tensor.transpose(dh[:, j, :], gated[:, j, :], ident[:])
+                    part = slice(half_pair * PASS, (half_pair + 1) * PASS)
+                    nc.vector.scalar_tensor_tensor(
+                        partial[:, part].rearrange("p (s j) -> p s j", j=PACK),
+                        tanh_half[:, part].rearrange("p (s j) -> p s j", j=PACK),
+                        1.0,
+                        dh[:].rearrange("p j s -> p s j"),
+                        ALU.add,
+                        ALU.mult,
+                    )
+                da = ring.tile([P, PAIR], BF16, name="da", align_bytes=64)
+                nc.vector.scalar_tensor_tensor(da[:], silu_neg[:], 1.0, partial[:], ALU.subtract, ALU.mult)
+                nc.vector.quantize_mx(
+                    out=da_codes[:, slots].bitcast(E5M2X4), scales=da_scales[:, slots], in_=da[:]
+                )
+                if pair == 0 and u + 1 < len(units):
+                    w2_q[units[u + 1]] = quantised(w2_raw[units[u + 1]], PASS, "w2", nc.scalar.copy)
+                if pair == 0:
+                    w1_codes, w1_scales = quantised(w1_raw[e, h], K, "w1", nc.vector.tensor_copy)
+                if e > 0 and pair == 0 and h == 0:
+                    scatter(e - 1, 0)
+            for kt in range(K_TILES):
+                cols = slice(kt * P, (kt + 1) * P)
+                if h == 0:
+                    dx[kt] = psum.tile([P, C], F32, name="dx", tag="dx")
+                nc.tensor.matmul_mx(
+                    out=dx[kt][:],
+                    lhsT=w1_codes[:, cols].bitcast(E4M3X4),
+                    lhsT_scale=w1_scales[:, cols],
+                    rhs=da_codes[:].bitcast(E5M2X4),
+                    rhs_scale=da_scales[:],
+                    start=(h == 0),
+                    stop=(h == HALVES - 1),
+                )
+            if h == HALVES - 1:
+                for kt in range(K_TILES):
+                    results[e, kt] = ring.tile([P, C], F32, name="result", bufs=E * K_TILES)
+                    nc.scalar.copy(results[e, kt][:], dx[kt][:])
+
+        windows[1] = ring.tile([P, T], F32, name="window1", tag="partial", bufs=1)
+        scatter(0, 1)
+        for kt in range(K_TILES):
+            scatter(E - 1, kt)
+            nc.sync.dma_start(out[kt * P : (kt + 1) * P, :], windows[kt][:])

@@ -17,6 +17,8 @@ E5M2X4 = mybir.dt.float8_e5m2_x4
 ACT = mybir.ActivationFunctionType
 ALU = mybir.AluOpType
 
+W1V = 2
+W2V = 2
 P = 128
 PACK = 4
 PASS = P * PACK
@@ -52,17 +54,15 @@ def tile_moe_bdx_mlp_silu_kernel(
         nc.sync.dma_start(words[:].bitcast(I32), dy_words[0].rearrange("p t d -> p (t d)").bitcast(I32))
 
         plane = keep.tile([P, T], U8, name="plane", align_bytes=64)
-        nc.vector.memset(plane[:].bitcast(I32), 0)
+        nc.gpsimd.memset(plane[:].bitcast(I32), 0)
         for r in range(4):
-            nc.sync.dma_start(plane[:].bitcast(I32)[r:P:32, :], dy_scales[0].bitcast(I32)[r:16:4, :])
+            nc.scalar.dma_start(plane[:].bitcast(I32)[r:P:32, :], dy_scales[0].bitcast(I32)[r:16:4, :])
 
         gate_rows = keep.tile([P, P], F32, name="gate_rows")
-        nc.vector.memset(gate_rows[:], 0.0)
+        nc.gpsimd.memset(gate_rows[:], 0.0)
+        nc.scalar.dma_start(gate_rows[0 : E * BLOCKS, :], gate[0:1, :].rearrange("o (b c) -> (o b) c", c=P))
         ident = keep.tile([P, P], F32, name="ident")
         make_identity(nc, ident[:])
-
-        warm = keep.tile([P, 1], F32, name="warm")
-        nc.scalar.activation(warm[:], ident[:, 0:1], ACT.Silu)
 
         w2_raw, a_raw, w1_raw = {}, {}, {}
 
@@ -75,32 +75,36 @@ def tile_moe_bdx_mlp_silu_kernel(
                 a_raw[e, h, first + pair] = tile[:, :, pair * PAIR_SLOTS : (pair + 1) * PAIR_SLOTS]
 
         def load_w2(e, h):
-            w2_raw[e, h] = keep.tile([P, PACK, PASS], F32, name="w2_raw%d%d" % (e, h))
+            w2_raw[e, h] = keep.tile([P, PACK, PASS], F32, name="w2_raw%d%d" % (e, h), align_bytes=64)
             cols = w2[e, :, h * PASS : (h + 1) * PASS]
             nc.sync.dma_start(w2_raw[e, h][:], cols.rearrange("(p j) i -> p j i", j=PACK))
 
-        def load_w1(e, h):
-            w1_raw[e, h] = keep.tile([P, PACK, K], F32, name="w1_raw%d%d" % (e, h))
-            rows = w1[e, h * PASS : (h + 1) * PASS, :]
-            nc.sync.dma_start(w1_raw[e, h][:], rows.rearrange("(p j) k -> p j k", j=PACK))
+        def load_w1(e):
+            w1_raw[e] = keep.tile([P, HALVES, PACK, K], F32, name="w1_raw%d" % e)
+            nc.sync.dma_start(w1_raw[e][:], w1[e].rearrange("(h p j) k -> p h j k", h=HALVES, j=PACK))
 
         load_a(*units[0], 0, 1)
         load_w2(*units[0])
-        nc.sync.dma_start(gate_rows[0 : E * BLOCKS, :], gate[0:1, :].rearrange("o (b c) -> (o b) c", c=P))
         load_a(*units[0], 1, 1)
-        for u in range(1, len(units)):
-            load_a(*units[u], 0, PAIRS)
-            load_w2(*units[u])
-            load_w1(*units[u - 1])
-        load_w1(*units[-1])
+        load_w2(*units[1])
+        load_a(*units[1], 0, PAIRS)
+        load_w1(0)
+        load_w2(*units[2])
+        load_a(*units[2], 0, PAIRS)
+        load_w2(*units[3])
+        load_a(*units[3], 0, PAIRS)
+        load_w1(1)
 
         lists = [offsets[:, e * C // 16 : (e + 1) * C // 16] for e in range(E)]
-        g_words = [keep.tile([P, C], U32, name="g_words%d" % e, align_bytes=64) for e in range(E)]
-        g_scales = [keep.tile([P, C], U8, name="g_scales%d" % e, align_bytes=64) for e in range(E)]
-        for e in range(E):
+        g_words, g_scales = {}, {}
+
+        def gather(e, words_tag, scales_tag):
+            g_words[e] = keep.tile([P, C], U32, name="g_words%d" % e, tag=words_tag, align_bytes=64)
             nc.vector.tensor_copy(g_words[e][:], words[:].indirect(lists[e]))
-        for e in range(E):
+            g_scales[e] = keep.tile([P, C], U8, name="g_scales%d" % e, tag=scales_tag, align_bytes=64)
             nc.vector.tensor_copy(g_scales[e][:], plane[:].indirect(lists[e]))
+
+        gather(0, "g_words0", "g_scales0")
 
         gate_t = psum.tile([P, C], F32, name="gate_t", tag="dx")
         nc.tensor.transpose(gate_t[:, 0:P], gate_rows[:], ident[:])
@@ -109,17 +113,37 @@ def tile_moe_bdx_mlp_silu_kernel(
 
         windows = {0: keep.tile([P, T], F32, name="window0")}
 
-        def quantised(raw, width, name, cast):
-            rounded = ring.tile([P, width * PACK], BF16, name=name + "_bf16", align_bytes=64)
+        def quantised(raw, width, name, cast, pool=ring):
+            rounded = pool.tile([P, width * PACK], BF16, name=name + "_bf16", align_bytes=64)
             cast(*interleaved(rounded[:], raw[:]))
             codes = ring.tile([P, width], U32, name=name + "_codes", align_bytes=64)
             scales = ring.tile([P, width], U8, name=name + "_scales", align_bytes=64)
             nc.vector.quantize_mx(out=codes[:].bitcast(E4M3X4), scales=scales[:], in_=rounded[:])
             return codes, scales
 
-        w2_q = {units[0]: quantised(w2_raw[units[0]], PASS, "w2", nc.vector.tensor_copy)}
+        def quantised_w1(e):
+            rounded = ring.tile([P, HALVES, K * PACK], BF16, name="w1_bf16", align_bytes=64)
+            cast = nc.vector.tensor_copy if e < W1V else nc.scalar.copy
+            cast(
+                rounded[:].rearrange("p h (c i j) -> p h c j i", i=4, j=PACK),
+                w1_raw[e][:].rearrange("p h j (c i) -> p h c j i", i=4),
+            )
+            codes = ring.tile([P, HALVES * K], U32, name="w1_codes", align_bytes=64)
+            scales = ring.tile([P, HALVES * K], U8, name="w1_scales", align_bytes=64)
+            nc.vector.quantize_mx(
+                out=codes[:].bitcast(E4M3X4), scales=scales[:], in_=rounded[:].rearrange("p h x -> p (h x)")
+            )
+            return codes, scales
+
+        w2_q = {units[0]: quantised(w2_raw[units[0]], PASS, "w2", nc.vector.tensor_copy, keep)}
+        gather(1, "g_words1", "w2_bf16")
         dx = {}
         results = {}
+
+        def silu_of_negated(pre):
+            values = ring.tile([P, PAIR], F32, name="silu_neg", bufs=4)
+            nc.scalar.activation(*interleaved(values[:], pre), ACT.Silu, scale=-1.0)
+            return values
 
         def scatter(e, kt):
             nc.vector.tensor_copy(windows[kt][:].indirect(lists[e]), results[e, kt][:])
@@ -130,12 +154,11 @@ def tile_moe_bdx_mlp_silu_kernel(
             da_scales = ring.tile([P, C], U8, name="da_scales", align_bytes=64)
             for pair in range(BLOCKS // 2):
                 slots = slice(pair * 2 * P, (pair + 1) * 2 * P)
+                if u == 0 and pair == 0:
+                    silu_neg = silu_of_negated(a_raw[e, h, pair])
                 tanh_half = ring.tile([P, PAIR], F32, name="tanh_half", bufs=4)
                 dst, src = interleaved(tanh_half[:], a_raw[e, h, pair])
                 nc.scalar.activation(dst, src, ACT.Tanh, scale=0.5)
-                silu_neg = ring.tile([P, PAIR], F32, name="silu_neg", bufs=4)
-                dst, src = interleaved(silu_neg[:], a_raw[e, h, pair])
-                nc.scalar.activation(dst, src, ACT.Silu, scale=-1.0)
                 last = u + 1 == len(units) and pair + 1 == PAIRS
                 if last:
                     partial = ring.tile([P, PAIR], F32, name="partial_last", tag="partial", bufs=1)
@@ -174,19 +197,21 @@ def tile_moe_bdx_mlp_silu_kernel(
                         ALU.add,
                         ALU.mult,
                     )
+                if u > 0 or pair > 0:
+                    silu_neg = silu_of_negated(a_raw[e, h, pair])
                 da = ring.tile([P, PAIR], BF16, name="da", align_bytes=64)
                 nc.vector.scalar_tensor_tensor(da[:], silu_neg[:], 1.0, partial[:], ALU.subtract, ALU.mult)
                 nc.vector.quantize_mx(
                     out=da_codes[:, slots].bitcast(E5M2X4), scales=da_scales[:, slots], in_=da[:]
                 )
                 if pair == 0 and u + 1 < len(units):
-                    w2_q[units[u + 1]] = quantised(w2_raw[units[u + 1]], PASS, "w2", nc.scalar.copy)
-                if pair == 0:
-                    w1_codes, w1_scales = quantised(w1_raw[e, h], K, "w1", nc.vector.tensor_copy)
+                    w2_q[units[u + 1]] = quantised(w2_raw[units[u + 1]], PASS, "w2", nc.vector.tensor_copy if u + 1 < W2V else nc.scalar.copy)
+                if pair == 0 and h == 0:
+                    w1_codes, w1_scales = quantised_w1(e)
                 if e > 0 and pair == 0 and h == 0:
                     scatter(e - 1, 0)
             for kt in range(K_TILES):
-                cols = slice(kt * P, (kt + 1) * P)
+                cols = slice(h * K + kt * P, h * K + (kt + 1) * P)
                 if h == 0:
                     dx[kt] = psum.tile([P, C], F32, name="dx", tag="dx")
                 nc.tensor.matmul_mx(

@@ -17,7 +17,7 @@ E5M2X4 = mybir.dt.float8_e5m2_x4
 ACT = mybir.ActivationFunctionType
 ALU = mybir.AluOpType
 
-W1V = 2
+W1V = 1
 W2V = 2
 P = 128
 PACK = 4
@@ -122,22 +122,45 @@ def tile_moe_bdx_mlp_silu_kernel(
             return codes, scales
 
         def quantised_w1(e):
-            rounded = ring.tile([P, HALVES, K * PACK], BF16, name="w1_bf16", align_bytes=64)
+            rounded = keep.tile([P, HALVES, K * PACK], BF16, name="w1_bf16_%d" % e, align_bytes=64)
             cast = nc.vector.tensor_copy if e < W1V else nc.scalar.copy
             cast(
                 rounded[:].rearrange("p h (c i j) -> p h c j i", i=4, j=PACK),
                 w1_raw[e][:].rearrange("p h j (c i) -> p h c j i", i=4),
             )
-            codes = ring.tile([P, HALVES * K], U32, name="w1_codes", align_bytes=64)
+            return rounded
+
+        def w1_codes_over(rounded, tag):
+            codes = keep.tile([P, HALVES * K], U32, name="w1_codes", tag=tag, align_bytes=64)
             scales = ring.tile([P, HALVES * K], U8, name="w1_scales", align_bytes=64)
             nc.vector.quantize_mx(
                 out=codes[:].bitcast(E4M3X4), scales=scales[:], in_=rounded[:].rearrange("p h x -> p (h x)")
             )
             return codes, scales
 
+        def second_product(e):
+            w1_codes, w1_scales = w1_q[e]
+            for kt in range(K_TILES):
+                dx = psum.tile([P, C], F32, name="dx", tag="dx")
+                for h in range(HALVES):
+                    da_codes, da_scales = da_q[e, h]
+                    cols = slice(h * K + kt * P, h * K + (kt + 1) * P)
+                    nc.tensor.matmul_mx(
+                        out=dx[:],
+                        lhsT=w1_codes[:, cols].bitcast(E4M3X4),
+                        lhsT_scale=w1_scales[:, cols],
+                        rhs=da_codes[:].bitcast(E5M2X4),
+                        rhs_scale=da_scales[:],
+                        start=(h == 0),
+                        stop=(h == HALVES - 1),
+                    )
+                results[e, kt] = ring.tile([P, C], F32, name="result", bufs=E * K_TILES)
+                nc.scalar.copy(results[e, kt][:], dx[:])
+
+        w1_q, da_q, w1_rounded = {}, {}, {}
+
         w2_q = {units[0]: quantised(w2_raw[units[0]], PASS, "w2", nc.vector.tensor_copy, keep)}
         gather(1, "g_words1", "w2_bf16")
-        dx = {}
         results = {}
 
         def silu_of_negated(pre):
@@ -150,8 +173,9 @@ def tile_moe_bdx_mlp_silu_kernel(
 
         for u, (e, h) in enumerate(units):
             w2_codes, w2_scales = w2_q[e, h]
-            da_codes = ring.tile([P, C], U32, name="da_codes", align_bytes=64)
-            da_scales = ring.tile([P, C], U8, name="da_scales", align_bytes=64)
+            da_codes = ring.tile([P, C], U32, name="da_codes", bufs=4, align_bytes=64)
+            da_scales = ring.tile([P, C], U8, name="da_scales", bufs=4, align_bytes=64)
+            da_q[e, h] = (da_codes, da_scales)
             for pair in range(BLOCKS // 2):
                 slots = slice(pair * 2 * P, (pair + 1) * 2 * P)
                 if u == 0 and pair == 0:
@@ -159,11 +183,7 @@ def tile_moe_bdx_mlp_silu_kernel(
                 tanh_half = ring.tile([P, PAIR], F32, name="tanh_half", bufs=4)
                 dst, src = interleaved(tanh_half[:], a_raw[e, h, pair])
                 nc.scalar.activation(dst, src, ACT.Tanh, scale=0.5)
-                last = u + 1 == len(units) and pair + 1 == PAIRS
-                if last:
-                    partial = ring.tile([P, PAIR], F32, name="partial_last", tag="partial", bufs=1)
-                else:
-                    partial = ring.tile([P, PAIR], F32, name="partial_ring")
+                partial = ring.tile([P, PAIR], F32, name="partial")
                 for half_pair in range(2):
                     b = 2 * pair + half_pair
                     cols = slice(b * P, (b + 1) * P)
@@ -206,29 +226,16 @@ def tile_moe_bdx_mlp_silu_kernel(
                 )
                 if pair == 0 and u + 1 < len(units):
                     w2_q[units[u + 1]] = quantised(w2_raw[units[u + 1]], PASS, "w2", nc.vector.tensor_copy if u + 1 < W2V else nc.scalar.copy)
-                if pair == 0 and h == 0:
-                    w1_codes, w1_scales = quantised_w1(e)
-                if e > 0 and pair == 0 and h == 0:
-                    scatter(e - 1, 0)
-            for kt in range(K_TILES):
-                cols = slice(h * K + kt * P, h * K + (kt + 1) * P)
-                if h == 0:
-                    dx[kt] = psum.tile([P, C], F32, name="dx", tag="dx")
-                nc.tensor.matmul_mx(
-                    out=dx[kt][:],
-                    lhsT=w1_codes[:, cols].bitcast(E4M3X4),
-                    lhsT_scale=w1_scales[:, cols],
-                    rhs=da_codes[:].bitcast(E5M2X4),
-                    rhs_scale=da_scales[:],
-                    start=(h == 0),
-                    stop=(h == HALVES - 1),
-                )
-            if h == HALVES - 1:
-                for kt in range(K_TILES):
-                    results[e, kt] = ring.tile([P, C], F32, name="result", bufs=E * K_TILES)
-                    nc.scalar.copy(results[e, kt][:], dx[kt][:])
+                if (u, pair) == (0, 0):
+                    w1_q[0] = w1_codes_over(quantised_w1(0), "w1_codes0")
+                if (u, pair) == (1, 1):
+                    second_product(0)
+                if (u, pair) == (2, 0):
+                    scatter(0, 0)
 
-        windows[1] = ring.tile([P, T], F32, name="window1", tag="partial", bufs=1)
+        w1_q[1] = w1_codes_over(quantised_w1(1), "w1_codes1")
+        second_product(1)
+        windows[1] = keep.tile([P, T], F32, name="window1", tag="w1_bf16_1", align_bytes=64)
         scatter(0, 1)
         for kt in range(K_TILES):
             scatter(E - 1, kt)

@@ -51,7 +51,6 @@ def tile_moe_bdx_mlp_silu_kernel(
         offsets = keep.tile([P, T // 16], U16, name="offsets")
         nc.sync.dma_start(offsets[:], offs)
         words = keep.tile([P, T], U32, name="words")
-        nc.sync.dma_start(words[:].bitcast(I32), dy_words[0].rearrange("p t d -> p (t d)").bitcast(I32))
 
         plane = keep.tile([P, T], U8, name="plane", align_bytes=64)
         nc.gpsimd.memset(plane[:].bitcast(I32), 0)
@@ -83,6 +82,7 @@ def tile_moe_bdx_mlp_silu_kernel(
             w1_raw[e] = keep.tile([P, HALVES, PACK, K], F32, name="w1_raw%d" % e)
             nc.sync.dma_start(w1_raw[e][:], w1[e].rearrange("(h p j) k -> p h j k", h=HALVES, j=PACK))
 
+        nc.sync.dma_start(words[:].bitcast(I32), dy_words[0].rearrange("p t d -> p (t d)").bitcast(I32))
         load_a(*units[0], 0, 1)
         load_w2(*units[0])
         load_a(*units[0], 1, 1)
@@ -121,30 +121,21 @@ def tile_moe_bdx_mlp_silu_kernel(
             nc.vector.quantize_mx(out=codes[:].bitcast(E4M3X4), scales=scales[:], in_=rounded[:])
             return codes, scales
 
-        def quantised_w1(e):
-            rounded = keep.tile([P, HALVES, K * PACK], BF16, name="w1_bf16_%d" % e, align_bytes=64)
-            cast = nc.vector.tensor_copy if e < W1V else nc.scalar.copy
-            cast(
-                rounded[:].rearrange("p h (c i j) -> p h c j i", i=4, j=PACK),
-                w1_raw[e][:].rearrange("p h j (c i) -> p h c j i", i=4),
-            )
-            return rounded
-
-        def w1_codes_over(rounded, tag):
-            codes = keep.tile([P, HALVES * K], U32, name="w1_codes", tag=tag, align_bytes=64)
-            scales = ring.tile([P, HALVES * K], U8, name="w1_scales", align_bytes=64)
-            nc.vector.quantize_mx(
-                out=codes[:].bitcast(E4M3X4), scales=scales[:], in_=rounded[:].rearrange("p h x -> p (h x)")
-            )
-            return codes, scales
+        def quantised_w1(e, h, cast, tag):
+            rounded = keep.tile([P, K * PACK], BF16, name="w1_bf16", tag=tag, align_bytes=64)
+            cast(*interleaved(rounded[:], w1_raw[e][:, h]))
+            codes = keep.tile([P, K], U32, name="w1_codes%d%d" % (e, h), align_bytes=64)
+            scales = keep.tile([P, K], U8, name="w1_scales%d%d" % (e, h), align_bytes=64)
+            nc.vector.quantize_mx(out=codes[:].bitcast(E4M3X4), scales=scales[:], in_=rounded[:])
+            w1_q[e, h] = (codes, scales)
 
         def second_product(e):
-            w1_codes, w1_scales = w1_q[e]
             for kt in range(K_TILES):
                 dx = psum.tile([P, C], F32, name="dx", tag="dx")
                 for h in range(HALVES):
                     da_codes, da_scales = da_q[e, h]
-                    cols = slice(h * K + kt * P, h * K + (kt + 1) * P)
+                    w1_codes, w1_scales = w1_q[e, h]
+                    cols = slice(kt * P, (kt + 1) * P)
                     nc.tensor.matmul_mx(
                         out=dx[:],
                         lhsT=w1_codes[:, cols].bitcast(E4M3X4),
@@ -157,7 +148,9 @@ def tile_moe_bdx_mlp_silu_kernel(
                 results[e, kt] = ring.tile([P, C], F32, name="result", bufs=E * K_TILES)
                 nc.scalar.copy(results[e, kt][:], dx[:])
 
-        w1_q, da_q, w1_rounded = {}, {}, {}
+        w1_q, da_q = {}, {}
+        V, S = nc.vector.tensor_copy, nc.scalar.copy
+        ENG = (V, V, V)
 
         w2_q = {units[0]: quantised(w2_raw[units[0]], PASS, "w2", nc.vector.tensor_copy, keep)}
         gather(1, "g_words1", "w2_bf16")
@@ -227,15 +220,20 @@ def tile_moe_bdx_mlp_silu_kernel(
                 if pair == 0 and u + 1 < len(units):
                     w2_q[units[u + 1]] = quantised(w2_raw[units[u + 1]], PASS, "w2", nc.vector.tensor_copy if u + 1 < W2V else nc.scalar.copy)
                 if (u, pair) == (0, 0):
-                    w1_q[0] = w1_codes_over(quantised_w1(0), "w1_codes0")
+                    quantised_w1(0, 0, ENG[0], "w1r00")
+                    quantised_w1(0, 1, ENG[1], "w1r01")
+                if (u, pair) == (2, 0) and ENG[2] is not None:
+                    quantised_w1(1, 0, ENG[2], "w1r10")
                 if (u, pair) == (1, 1):
                     second_product(0)
                 if (u, pair) == (2, 0):
                     scatter(0, 0)
 
-        w1_q[1] = w1_codes_over(quantised_w1(1), "w1_codes1")
+        if ENG[2] is None:
+            quantised_w1(1, 0, nc.scalar.copy, "w1r10")
+        quantised_w1(1, 1, nc.scalar.copy, "w1r11")
         second_product(1)
-        windows[1] = keep.tile([P, T], F32, name="window1", tag="w1_bf16_1", align_bytes=64)
+        windows[1] = keep.tile([P, T], F32, name="window1", tag="w1r11", align_bytes=64)
         scatter(0, 1)
         for kt in range(K_TILES):
             scatter(E - 1, kt)

from contextlib import ExitStack

import concourse.mybir as mybir
from concourse.masks import make_identity

K, T, E, C, H, N = 256, 1024, 2, 512, 1024, 512
FLOPS = 2 * E * C * (N * H + H * K)

F32 = mybir.dt.float32
BF16 = mybir.dt.bfloat16
I32 = mybir.dt.int32
U32 = mybir.dt.uint32
U16 = mybir.dt.uint16
U8 = mybir.dt.uint8
E4M3X4 = mybir.dt.float8_e4m3fn_x4
E5M2X4 = mybir.dt.float8_e5m2_x4
ACT = mybir.ActivationFunctionType
ALU = mybir.AluOpType

W1V = 1
W2V = 2
P = 128
PACK = 4
PASS = P * PACK
HALVES = H // PASS
BLOCKS = C // P
K_TILES = K // P
PAIRS = BLOCKS // 2
PAIR_SLOTS = 2 * P
PAIR = PAIR_SLOTS * PACK


def interleaved(dst, src):
    return (
        dst.rearrange("p (c i j) -> p c j i", i=4, j=PACK),
        src.rearrange("p j (c i) -> p c j i", i=4),
    )


def tile_moe_bdx_mlp_silu_kernel(
    tc, dy_words, dy_scales, a, w2, w1, gate, offs, out
):
    nc = tc.nc
    units = [(e, h) for e in range(E) for h in range(HALVES)]

    with ExitStack() as ctx:
        keep = ctx.enter_context(tc.tile_pool(name="keep", bufs=1))
        ring = ctx.enter_context(tc.tile_pool(name="ring", bufs=2))
        psum = ctx.enter_context(tc.psum_pool(name="psum", bufs=2))

        offsets = keep.tile([P, T // 16], U16, name="offsets")
        nc.sync.dma_start(offsets[:], offs)
        words = keep.tile([P, T], U32, name="words")

        plane = keep.tile([P, T], U8, name="plane", align_bytes=64)
        nc.gpsimd.memset(plane[:].bitcast(I32), 0)
        for r in range(4):
            nc.scalar.dma_start(plane[:].bitcast(I32)[r:P:32, :], dy_scales[0].bitcast(I32)[r:16:4, :])

        gate_rows = keep.tile([P, P], F32, name="gate_rows")
        nc.gpsimd.memset(gate_rows[:], 0.0)
        nc.scalar.dma_start(gate_rows[0 : E * BLOCKS, :], gate[0:1, :].rearrange("o (b c) -> (o b) c", c=P))
        ident = keep.tile([P, P], F32, name="ident")
        make_identity(nc, ident[:])

        w2_raw, a_raw, w1_raw = {}, {}, {}

        def load_a(e, h, first, count):
            tile = keep.tile([P, PACK, count * PAIR_SLOTS], F32, name="a_raw%d%d%d" % (e, h, first))
            lo = e * C + first * PAIR_SLOTS
            rows = a[h * PASS : (h + 1) * PASS, lo : lo + count * PAIR_SLOTS]
            nc.sync.dma_start(tile[:], rows.rearrange("(p j) s -> p j s", j=PACK))
            for pair in range(count):
                a_raw[e, h, first + pair] = tile[:, :, pair * PAIR_SLOTS : (pair + 1) * PAIR_SLOTS]

        def load_w2(e, h):
            w2_raw[e, h] = keep.tile([P, PACK, PASS], F32, name="w2_raw%d%d" % (e, h), align_bytes=64)
            cols = w2[e, :, h * PASS : (h + 1) * PASS]
            nc.sync.dma_start(w2_raw[e, h][:], cols.rearrange("(p j) i -> p j i", j=PACK))

        def load_w1(e):
            w1_raw[e] = keep.tile([P, HALVES, PACK, K], F32, name="w1_raw%d" % e)
            nc.sync.dma_start(w1_raw[e][:], w1[e].rearrange("(h p j) k -> p h j k", h=HALVES, j=PACK))

        nc.sync.dma_start(words[:].bitcast(I32), dy_words[0].rearrange("p t d -> p (t d)").bitcast(I32))
        load_a(*units[0], 0, 1)
        load_w2(*units[0])
        load_a(*units[0], 1, 1)
        load_w2(*units[1])
        load_a(*units[1], 0, PAIRS)
        load_w1(0)
        load_w2(*units[2])
        load_a(*units[2], 0, PAIRS)
        load_w2(*units[3])
        load_a(*units[3], 0, PAIRS)
        load_w1(1)

        lists = [offsets[:, e * C // 16 : (e + 1) * C // 16] for e in range(E)]
        g_words, g_scales = {}, {}

        def gather(e, words_tag, scales_tag):
            g_words[e] = keep.tile([P, C], U32, name="g_words%d" % e, tag=words_tag, align_bytes=64)
            nc.vector.tensor_copy(g_words[e][:], words[:].indirect(lists[e]))
            g_scales[e] = keep.tile([P, C], U8, name="g_scales%d" % e, tag=scales_tag, align_bytes=64)
            nc.vector.tensor_copy(g_scales[e][:], plane[:].indirect(lists[e]))

        gather(0, "g_words0", "g_scales0")

        gate_t = psum.tile([P, C], F32, name="gate_t", tag="dx")
        nc.tensor.transpose(gate_t[:, 0:P], gate_rows[:], ident[:])
        gate_col = keep.tile([P, E * BLOCKS], F32, name="gate_col")
        nc.vector.tensor_scalar(gate_col[:], gate_t[:, 0 : E * BLOCKS], -0.5, None, ALU.mult)

        windows = {0: keep.tile([P, T], F32, name="window0")}

        def quantised(raw, width, name, cast, pool=ring):
            rounded = pool.tile([P, width * PACK], BF16, name=name + "_bf16", align_bytes=64)
            cast(*interleaved(rounded[:], raw[:]))
            codes = ring.tile([P, width], U32, name=name + "_codes", align_bytes=64)
            scales = ring.tile([P, width], U8, name=name + "_scales", align_bytes=64)
            nc.vector.quantize_mx(out=codes[:].bitcast(E4M3X4), scales=scales[:], in_=rounded[:])
            return codes, scales

        def quantised_w1(e, h, cast, tag):
            rounded = keep.tile([P, K * PACK], BF16, name="w1_bf16", tag=tag, align_bytes=64)
            cast(*interleaved(rounded[:], w1_raw[e][:, h]))
            codes = keep.tile([P, K], U32, name="w1_codes%d%d" % (e, h), align_bytes=64)
            scales = keep.tile([P, K], U8, name="w1_scales%d%d" % (e, h), align_bytes=64)
            nc.vector.quantize_mx(out=codes[:].bitcast(E4M3X4), scales=scales[:], in_=rounded[:])
            w1_q[e, h] = (codes, scales)

        def second_product(e):
            for kt in range(K_TILES):
                dx = psum.tile([P, C], F32, name="dx", tag="dx")
                for h in range(HALVES):
                    da_codes, da_scales = da_q[e, h]
                    w1_codes, w1_scales = w1_q[e, h]
                    cols = slice(kt * P, (kt + 1) * P)
                    nc.tensor.matmul_mx(
                        out=dx[:],
                        lhsT=w1_codes[:, cols].bitcast(E4M3X4),
                        lhsT_scale=w1_scales[:, cols],
                        rhs=da_codes[:].bitcast(E5M2X4),
                        rhs_scale=da_scales[:],
                        start=(h == 0),
                        stop=(h == HALVES - 1),
                    )
                results[e, kt] = ring.tile([P, C], F32, name="result", bufs=E * K_TILES)
                nc.scalar.copy(results[e, kt][:], dx[:])

        w1_q, da_q = {}, {}
        V, S = nc.vector.tensor_copy, nc.scalar.copy
        ENG = (V, V, V)

        w2_q = {units[0]: quantised(w2_raw[units[0]], PASS, "w2", nc.vector.tensor_copy, keep)}
        gather(1, "g_words1", "w2_bf16")
        results = {}

        def silu_of_negated(pre):
            values = ring.tile([P, PAIR], F32, name="silu_neg", bufs=4)
            nc.scalar.activation(*interleaved(values[:], pre), ACT.Silu, scale=-1.0)
            return values

        def scatter(e, kt):
            nc.vector.tensor_copy(windows[kt][:].indirect(lists[e]), results[e, kt][:])

        for u, (e, h) in enumerate(units):
            w2_codes, w2_scales = w2_q[e, h]
            da_codes = ring.tile([P, C], U32, name="da_codes", bufs=4, align_bytes=64)
            da_scales = ring.tile([P, C], U8, name="da_scales", bufs=4, align_bytes=64)
            da_q[e, h] = (da_codes, da_scales)
            for pair in range(BLOCKS // 2):
                slots = slice(pair * 2 * P, (pair + 1) * 2 * P)
                if u == 0 and pair == 0:
                    silu_neg = silu_of_negated(a_raw[e, h, pair])
                tanh_half = ring.tile([P, PAIR], F32, name="tanh_half", bufs=4)
                dst, src = interleaved(tanh_half[:], a_raw[e, h, pair])
                nc.scalar.activation(dst, src, ACT.Tanh, scale=0.5)
                partial = ring.tile([P, PAIR], F32, name="partial")
                for half_pair in range(2):
                    b = 2 * pair + half_pair
                    cols = slice(b * P, (b + 1) * P)
                    dh_t = psum.tile([P, PASS], F32, name="dh_t", bufs=3)
                    nc.tensor.matmul_mx(
                        out=dh_t[:],
                        lhsT=g_words[e][:, cols].bitcast(E5M2X4),
                        lhsT_scale=g_scales[e][:, cols],
                        rhs=w2_codes[:].bitcast(E4M3X4),
                        rhs_scale=w2_scales[:],
                        start=True,
                        stop=True,
                    )
                    gated = ring.tile([P, PACK, P], F32, name="gated", bufs=3)
                    col = e * BLOCKS + b
                    nc.scalar.activation(
                        gated[:],
                        dh_t[:].rearrange("s (p j) -> s j p", j=PACK),
                        ACT.Copy,
                        scale=gate_col[:, col : col + 1],
                    )
                    dh = psum.tile([P, PACK, P], F32, name="dh", bufs=3)
                    for j in range(PACK):
                        nc.tensor.transpose(dh[:, j, :], gated[:, j, :], ident[:])
                    part = slice(half_pair * PASS, (half_pair + 1) * PASS)
                    nc.vector.scalar_tensor_tensor(
                        partial[:, part].rearrange("p (s j) -> p s j", j=PACK),
                        tanh_half[:, part].rearrange("p (s j) -> p s j", j=PACK),
                        1.0,
                        dh[:].rearrange("p j s -> p s j"),
                        ALU.add,
                        ALU.mult,
                    )
                if u > 0 or pair > 0:
                    silu_neg = silu_of_negated(a_raw[e, h, pair])
                da = ring.tile([P, PAIR], BF16, name="da", align_bytes=64)
                nc.vector.scalar_tensor_tensor(da[:], silu_neg[:], 1.0, partial[:], ALU.subtract, ALU.mult)
                nc.vector.quantize_mx(
                    out=da_codes[:, slots].bitcast(E5M2X4), scales=da_scales[:, slots], in_=da[:]
                )
                if pair == 0 and u + 1 < len(units):
                    w2_q[units[u + 1]] = quantised(w2_raw[units[u + 1]], PASS, "w2", nc.vector.tensor_copy if u + 1 < W2V else nc.scalar.copy)
                if (u, pair) == (0, 0):
                    quantised_w1(0, 0, ENG[0], "w1r00")
                    quantised_w1(0, 1, ENG[1], "w1r01")
                if (u, pair) == (2, 0) and ENG[2] is not None:
                    quantised_w1(1, 0, ENG[2], "w1r10")
                if (u, pair) == (1, 1):
                    second_product(0)
                if (u, pair) == (2, 0):
                    scatter(0, 0)

        if ENG[2] is None:
            quantised_w1(1, 0, nc.scalar.copy, "w1r10")
        quantised_w1(1, 1, nc.scalar.copy, "w1r11")
        second_product(1)
        windows[1] = keep.tile([P, T], F32, name="window1", tag="w1r11", align_bytes=64)
        scatter(0, 1)
        for kt in range(K_TILES):
            scatter(E - 1, kt)
            nc.sync.dma_start(out[kt * P : (kt + 1) * P, :], windows[kt][:])
